import numpy as np
import ml_dtypes


def mxq(x, axis, fmt="e4m3"):
    dtype, down = {"e4m3": (ml_dtypes.float8_e4m3fn, 7), "e5m2": (ml_dtypes.float8_e5m2, 14)}[fmt]
    v = np.moveaxis(np.asarray(x, np.float32).astype(ml_dtypes.bfloat16).astype(np.float64), axis, -1)
    blocks = v.reshape(v.shape[:-1] + (-1, 32))
    amax = np.abs(blocks).max(-1, keepdims=True)
    byte = np.maximum(np.where(amax > 0, np.frexp(amax)[1] - 1 + 127, 0) - down, 1)
    scale = np.exp2(byte - 127.0)
    codes = (blocks / scale).astype(np.float32).astype(dtype).astype(np.float64)
    return np.moveaxis((codes * scale).reshape(v.shape), -1, axis)


WIDE = False


def mx_kscale(k):
    if not WIDE:
        return np.ones(k)
    levels = np.array([10, -10, 5, -5, 0])
    if k % 512:
        return np.exp2(np.random.permutation(np.resize(levels, k // 32))).repeat(32)
    a = np.empty((k // 512, 16))
    for p in range(k // 512):
        a[p, :8] = np.random.permutation(np.resize(levels, 8))
        for g in range(8):
            far = levels[np.abs(levels - a[p, g]) >= 10]
            a[p, g + 8] = far[np.random.randint(len(far))]
    return np.exp2(a.ravel()).repeat(32)


def f64(x):
    return np.asarray(x).astype(np.float64)


def striped(idx):
    return np.tile(idx.reshape(-1, 16).T, (8, 1)).astype(np.uint16)


def unstriped(offs):
    return offs[:16].T.reshape(-1).astype(np.int64)


def striped8(idx):
    return np.concatenate([x.reshape(-1, 16).T for x in idx]).astype(np.uint16)


def runs(offs, k):
    lists = np.stack([offs[16 * r : 16 * r + 16].T.reshape(-1) for r in range(8)]).astype(np.int64)
    return lists[np.arange(k) % 512 // 64]


def pack_weight(w):
    k, n = w.shape
    w = f64(np.asarray(w, np.float32).astype(ml_dtypes.bfloat16)).reshape(k // 32, 32, n)
    amax = np.abs(w).max(1)
    byte = np.clip(np.where(amax > 0, np.frexp(amax)[1] - 1 + 127 - 7, 1), 1, 254)
    scaled = (w * np.exp2(127.0 - byte)[:, None, :]).reshape(k, n).astype(np.float32)
    words = np.ascontiguousarray(scaled.reshape(k // 512, 128, 4, n).transpose(0, 1, 3, 2)).astype(ml_dtypes.float8_e4m3fn).view(np.uint8)
    return words, np.ascontiguousarray(byte.astype(np.uint8).reshape(k // 512, 16, n))


def unpack_weight(words, scales):
    g, p, n, _ = words.shape
    vals = np.ascontiguousarray(words).view(ml_dtypes.float8_e4m3fn).astype(np.float64) * np.repeat(np.exp2(scales.astype(np.float64) - 127.0), 8, axis=1)[..., None]
    return vals.transpose(0, 1, 3, 2).reshape(g * 512, n)


def relu(v):
    return np.maximum(v, 0.0)


def sigmoid(v):
    return 1.0 / (1.0 + np.exp(-np.maximum(v, -700.0)))


K, T, S, N, H = 512, 2048, 512, 512, 512


def setup_inputs():
    n = np.random.standard_normal
    s = mx_kscale(K)[:, None]
    u = mx_kscale(H)
    packed_xT = pack_weight(n((K, T)) * s)
    return {
        "x_words": packed_xT[0],
        "x_scales": packed_xT[1],
        "w1": (n((K, H)) / np.sqrt(K) / s).astype(np.float32),
        "gn": (np.random.uniform(0.5, 1.5, (H, 1)) * u[:, None]).astype(np.float32),
        "gm": (np.random.uniform(0.5, 1.5, (H, 1)) * u[:, None]).astype(np.float32),
        "w2": (n((H, N)) / np.sqrt(2 * H) / u[:, None]).astype(np.float32),
        "w3": (n((H, N)) / np.sqrt(2 * H) / u[:, None]).astype(np.float32),
        "offs": striped(np.random.permutation(T)[:S]),
        "n1": striped8(np.stack([np.random.permutation(S) for _ in range(8)])),
        "n2": striped8(np.stack([np.random.permutation(S) for _ in range(8)])),
        "n3": striped8(np.stack([np.random.permutation(S) for _ in range(8)])),
        "n4": striped8(np.stack([np.random.permutation(S) for _ in range(8)])),
        "n5": striped8(np.stack([np.random.permutation(S) for _ in range(8)])),
        "n6": striped8(np.stack([np.random.permutation(S) for _ in range(8)])),
    }


def reference(x_words, x_scales, w1, gn, gm, w2, w3, offs, n1, n2, n3, n4, n5, n6):
    xq = unpack_weight(x_words, x_scales)[:, unstriped(offs)]
    y = mxq(f64(w1), 0, "e4m3").T @ xq
    rl = relu(y)
    ds = np.zeros((H, S))
    ds[np.arange(H)[:, None], runs(n1, H)] = rl
    z = f64(gn) * (ds - (0.5 * y))
    pa = y[np.arange(H)[:, None], runs(n2, H)]
    z2 = f64(gm) * (pa + (sigmoid(y[np.arange(H)[:, None], runs(n3, H)])) * (y[np.arange(H)[:, None], runs(n4, H)] - pa))
    h = mxq(f64(w2), 0, "e4m3").T @ mxq(z, 0, "e4m3") + mxq(f64(w3), 0, "e4m3").T @ mxq(z2, 0, "e4m3")
    return 0.75 * ((h - (h[np.arange(N)[:, None], runs(n5, N)])) * (h - (h[np.arange(N)[:, None], runs(n6, N)])))

@@ -1,0 +1,223 @@
+from contextlib import ExitStack
+
+import concourse.mybir as mybir
+
+K, T, S, N, H = 512, 2048, 512, 512, 512
+FLOPS = 2 * K * H * S + 2 * 2 * H * N * S
+
+F32 = mybir.dt.float32
+BF16 = mybir.dt.bfloat16
+I32 = mybir.dt.int32
+U32 = mybir.dt.uint32
+U16 = mybir.dt.uint16
+U8 = mybir.dt.uint8
+FP8X4 = mybir.dt.float8_e4m3fn_x4
+ALU = mybir.AluOpType
+ACT = mybir.ActivationFunctionType
+
+P = 128
+PACK = 4
+LIST_ROWS = 16
+BLOCKS = ((0, 256), (256, 384), (384, 512))
+
+
+def tile_picked_joinsendlerpquad_none_p_kernel(
+    tc, x_words, x_scales, w1, gn, gm, w2, w3, offs, n1, n2, n3, n4, n5, n6, out
+):
+    nc = tc.nc
+    with ExitStack() as ctx:
+        lists = ctx.enter_context(tc.tile_pool(name="lists", bufs=1))
+        keep = ctx.enter_context(tc.tile_pool(name="keep", bufs=1))
+        psum = ctx.enter_context(tc.psum_pool(name="psum", bufs=1))
+
+        def load_list(src, name):
+            dst = lists.tile([P, S // LIST_ROWS], U16, name=name)
+            nc.sync.dma_start(dst[:], src)
+            return dst
+
+        def load_weight(src, name):
+            dst = keep.tile([P, PACK, H], F32, name=name)
+            nc.sync.dma_start(dst[:], src.rearrange("(p j) c -> p j c", j=PACK))
+            return dst
+
+        def load_gain(src, name):
+            dst = keep.tile([P, PACK], F32, name=name)
+            nc.sync.dma_start(dst[:], src.rearrange("(p t) o -> p (t o)", t=PACK))
+            return dst
+
+        def entries(lst, lo, hi):
+            return lst[:, lo // LIST_ROWS : hi // LIST_ROWS]
+
+        x_bytes = keep.tile([P, T], U8, name="x_bytes", align_bytes=64)
+        nc.gpsimd.memset(x_bytes[:].bitcast(I32), 0)
+        for q in range(4):
+            nc.scalar.dma_start(
+                x_bytes[32 * q : 32 * q + 4, :].bitcast(I32), x_scales[0, 4 * q : 4 * q + 4, :].bitcast(I32)
+            )
+        warm = keep.tile([P, 1], F32, name="warm")
+        nc.vector.memset(warm[:], 0.0)
+        warm_out = keep.tile([P, 1], F32, name="warm_out")
+        nc.scalar.activation(warm_out[:], warm[:], ACT.Sigmoid)
+
+        offs_sb = load_list(offs, "offs_sb")
+        gn_sb = load_gain(gn, "gn_sb")
+        w1_raw = load_weight(w1, "w1_raw")
+        x_codes = keep.tile([P, T], U32, name="x_codes", align_bytes=64)
+        nc.sync.dma_start(x_codes[:].bitcast(I32), x_words[0].rearrange("p n t -> p (n t)").bitcast(I32))
+        n1_sb = load_list(n1, "n1_sb")
+        gm_sb = load_gain(gm, "gm_sb")
+        n3_sb = load_list(n3, "n3_sb")
+        w2_raw = load_weight(w2, "w2_raw")
+        w3_raw = load_weight(w3, "w3_raw")
+        n2_sb = load_list(n2, "n2_sb")
+        n4_sb = load_list(n4, "n4_sb")
+        n5_sb = load_list(n5, "n5_sb")
+        n6_sb = load_list(n6, "n6_sb")
+
+        gn_full = keep.tile([P, PACK, S], F32, name="gn_full")
+        nc.scalar.copy(gn_full[:], gn_sb[:].unsqueeze(2).to_broadcast([P, PACK, S]))
+        gn_half = keep.tile([P, PACK], F32, name="gn_half")
+        nc.vector.tensor_scalar(gn_half[:], gn_sb[:], -0.5, None, ALU.mult)
+
+        xg_codes = keep.tile([P, S], U32, name="xg_codes", align_bytes=64)
+        xg_bytes = keep.tile([P, S], U8, name="xg_bytes", align_bytes=64)
+        nc.vector.tensor_copy(xg_bytes[:], x_bytes[:].indirect(offs_sb[:]))
+
+        def deal(copy, raw, t0, t1, name):
+            nt = t1 - t0
+            dealt = keep.tile([P, nt * P * PACK], BF16, name=name, align_bytes=64)
+            copy(
+                dealt[:].rearrange("p (t m j) -> p m j t", t=nt, j=PACK),
+                raw[:].rearrange("p j (m t) -> p m j t", t=PACK)[:, :, :, t0:t1],
+            )
+            return dealt
+
+        def quantize(src, name):
+            width = src.shape[1] // PACK
+            codes = keep.tile([P, width], U32, name=name + "_codes", align_bytes=64)
+            scales = keep.tile([P, width], U8, name=name + "_scales", align_bytes=64)
+            nc.vector.quantize_mx(out=codes[:].bitcast(FP8X4), scales=scales[:], in_=src)
+            return codes[:], scales[:]
+
+        def mm(dst, stationary, m, moving, start, stop):
+            cols = slice(m * P, (m + 1) * P)
+            nc.tensor.matmul_mx(
+                out=dst,
+                lhsT=stationary[0][:, cols].bitcast(FP8X4),
+                lhsT_scale=stationary[1][:, cols],
+                rhs=moving[0].bitcast(FP8X4),
+                rhs_scale=moving[1],
+                start=start,
+                stop=stop,
+            )
+
+        w1_lo = deal(nc.vector.tensor_copy, w1_raw, 0, 2, "w1_lo")
+        w1_hi = deal(nc.scalar.copy, w1_raw, 2, 4, "w1_hi")
+        w1_q = [quantize(w1_lo[:], "w1_lo"), quantize(w1_hi[:], "w1_hi")]
+        halves = ((0, S // 2), (S // 2, S))
+        for lo, hi in halves:
+            nc.vector.tensor_copy(xg_codes[:, lo:hi], x_codes[:].indirect(entries(offs_sb, lo, hi)))
+
+        def pieces_of(t):
+            return halves if t == 0 else ((0, S),)
+
+        y_ps = [psum.tile([P, S], F32, name="y_ps%d" % t) for t in range(PACK)]
+        for t in range(PACK):
+            for lo, hi in pieces_of(t):
+                mm(y_ps[t][:, lo:hi], w1_q[t // 2], t % 2, (xg_codes[:, lo:hi], xg_bytes[:, lo:hi]), True, True)
+
+        rows = [keep.tile([P, 2 * S], F32, name="rows%d" % t) for t in range(PACK)]
+        y_gm = [keep.tile([P, S], F32, name="y_gm%d" % t) for t in range(PACK)]
+        ds = [keep.tile([P, 2 * S], F32, name="ds%d" % t) for t in range(PACK)]
+        sig = [keep.tile([P, S], F32, name="sig%d" % t) for t in range(PACK)]
+        cosig = [keep.tile([P, S], F32, name="cosig%d" % t) for t in range(PACK)]
+        z_planes = keep.tile([P, PACK, S], BF16, name="z_planes")
+
+        for t in range(PACK):
+            for lo, hi in pieces_of(t):
+                nc.scalar.activation(rows[t][:, S + lo : S + hi], y_ps[t][:, lo:hi], ACT.Relu)
+        for t in range(PACK):
+            nc.scalar.copy(rows[t][:, :S], y_ps[t][:])
+        w2_b = deal(nc.scalar.copy, w2_raw, 0, 4, "w2_b")
+        w3_b = deal(nc.scalar.copy, w3_raw, 0, 4, "w3_b")
+        for t in range(PACK):
+            for lo, hi in pieces_of(t):
+                nc.vector.tensor_tensor(
+                    ds[t][:].indirect(entries(n1_sb, lo, hi)),
+                    rows[t][:, S + lo : S + hi],
+                    gn_full[:, t, lo:hi],
+                    ALU.mult,
+                )
+        for t in range(PACK):
+            nc.vector.scalar_tensor_tensor(
+                z_planes[:, t, :], rows[t][:, :S], gn_half[:, t : t + 1], ds[t][:, :S], ALU.mult, ALU.add
+            )
+        w2_q = quantize(w2_b[:], "w2")
+        w3_q = quantize(w3_b[:], "w3")
+        for t in range(PACK):
+            nc.scalar.activation(y_gm[t][:], y_ps[t][:], ACT.Copy, scale=gm_sb[:, t : t + 1])
+            nc.scalar.activation(sig[t][:], rows[t][:].indirect(n3_sb[:]), ACT.Sigmoid)
+            nc.scalar.activation(cosig[t][:], sig[t][:], ACT.Copy, bias=1.0, scale=-1.0)
+
+        z_q = []
+        for b, (lo, hi) in enumerate(BLOCKS):
+            z_b = keep.tile([P, (hi - lo) * PACK], BF16, name="z_b%d" % b, align_bytes=64)
+            nc.scalar.copy(
+                z_b[:].rearrange("p (c i t) -> p c t i", i=4, t=PACK),
+                z_planes[:, :, lo:hi].rearrange("p t (c i) -> p c t i", i=4),
+            )
+            z_q.append(quantize(z_b[:], "zq%d" % b))
+
+        h_ps = [psum.tile([P, S], F32, name="h_ps%d" % m) for m in range(PACK)]
+        h_last = [psum.tile([P, S], F32, name="h_last%d" % m, tag="y_ps%d" % m) for m in range(PACK)]
+        h_plain = [keep.tile([P, S], F32, name="h_plain%d" % m) for m in range(PACK)]
+        for b, (lo, hi) in enumerate(BLOCKS):
+            n = hi - lo
+            last = b == len(BLOCKS) - 1
+            banks = h_last if last else h_ps
+            part_a = keep.tile([P, PACK, n], F32, name="part_a")
+            part_b = keep.tile([P, PACK, n], F32, name="part_b")
+            for t in range(PACK):
+                nc.vector.tensor_tensor(
+                    part_a[:, t, :], y_gm[t][:].indirect(entries(n2_sb, lo, hi)), cosig[t][:, lo:hi], ALU.mult
+                )
+                nc.vector.tensor_tensor(
+                    part_b[:, t, :], y_gm[t][:].indirect(entries(n4_sb, lo, hi)), sig[t][:, lo:hi], ALU.mult
+                )
+            z2_b = keep.tile([P, n * PACK], BF16, name="z2_b%d" % b, align_bytes=64)
+            nc.vector.tensor_tensor(
+                z2_b[:].rearrange("p (c i t) -> p c t i", i=4, t=PACK),
+                part_a[:].rearrange("p t (c i) -> p c t i", i=4),
+                part_b[:].rearrange("p t (c i) -> p c t i", i=4),
+                ALU.add,
+            )
+            z2_q = quantize(z2_b[:], "z2q%d" % b)
+            if last:
+                for m in range(PACK):
+                    mm(banks[m][:, lo:hi], w2_q, m, z_q[b], True, False)
+                for m in range(PACK):
+                    mm(banks[m][:, lo:hi], w3_q, m, z2_q, False, True)
+            else:
+                for m in range(PACK):
+                    mm(banks[m][:, lo:hi], w2_q, m, z_q[b], True, False)
+                    mm(banks[m][:, lo:hi], w3_q, m, z2_q, False, True)
+            for m in range(PACK):
+                nc.scalar.copy(rows[m][:, lo:hi], banks[m][:, lo:hi])
+                nc.scalar.copy(h_plain[m][:, lo:hi], banks[m][:, lo:hi])
+
+        out_rows = out.rearrange("(p t) j -> p t j", t=PACK)
+        for m in range(PACK):
+            pieces = ((0, S),) if m < PACK - 1 else ((0, S // 2), (S // 2, S))
+            for lo, hi in pieces:
+                n = hi - lo
+                d5 = keep.tile([P, n], F32, name="d5_%d_%d" % (m, lo))
+                d6 = keep.tile([P, n], F32, name="d6_%d_%d" % (m, lo))
+                res = keep.tile([P, n], F32, name="res_%d_%d" % (m, lo))
+                nc.vector.tensor_tensor(
+                    d5[:], rows[m][:].indirect(entries(n5_sb, lo, hi)), h_plain[m][:, lo:hi], ALU.subtract
+                )
+                nc.vector.tensor_tensor(
+                    d6[:], rows[m][:].indirect(entries(n6_sb, lo, hi)), h_plain[m][:, lo:hi], ALU.subtract
+                )
+                nc.vector.scalar_tensor_tensor(res[:], d5[:], 0.75, d6[:], ALU.mult, ALU.mult)
+                nc.sync.dma_start(out_rows[:, m, lo:hi], res[:])

@@ -1,6 +1,7 @@
 from contextlib import ExitStack
 
 import concourse.mybir as mybir
+from concourse.masks import make_identity
 
 K, T, S, N, H = 512, 2048, 512, 512, 512
 FLOPS = 2 * K * H * S + 2 * 2 * H * N * S
@@ -18,7 +19,7 @@ ACT = mybir.ActivationFunctionType
 P = 128
 PACK = 4
 LIST_ROWS = 16
-BLOCKS = ((0, 256), (256, 384), (384, 512))
+BLOCKS = ((0, 256), (256, 512))
 
 
 def tile_picked_joinsendlerpquad_none_p_kernel(
@@ -49,21 +50,25 @@ def tile_picked_joinsendlerpquad_none_p_kernel(
             return lst[:, lo // LIST_ROWS : hi // LIST_ROWS]
 
         x_bytes = keep.tile([P, T], U8, name="x_bytes", align_bytes=64)
-        nc.gpsimd.memset(x_bytes[:].bitcast(I32), 0)
-        for q in range(4):
-            nc.scalar.dma_start(
-                x_bytes[32 * q : 32 * q + 4, :].bitcast(I32), x_scales[0, 4 * q : 4 * q + 4, :].bitcast(I32)
-            )
+        nc.vector.memset(x_bytes[:, : T // 2].bitcast(I32), 0)
+        nc.gpsimd.memset(x_bytes[:, T // 2 :].bitcast(I32), 0)
         warm = keep.tile([P, 1], F32, name="warm")
         nc.vector.memset(warm[:], 0.0)
         warm_out = keep.tile([P, 1], F32, name="warm_out")
         nc.scalar.activation(warm_out[:], warm[:], ACT.Sigmoid)
 
-        offs_sb = load_list(offs, "offs_sb")
-        gn_sb = load_gain(gn, "gn_sb")
+        ident = keep.tile([P, P], F32, name="ident")
+        make_identity(nc, ident[:])
+
         w1_raw = load_weight(w1, "w1_raw")
+        offs_sb = load_list(offs, "offs_sb")
+        for q in range(4):
+            nc.sync.dma_start(
+                x_bytes[32 * q : 32 * q + 4, :].bitcast(I32), x_scales[0, 4 * q : 4 * q + 4, :].bitcast(I32)
+            )
         x_codes = keep.tile([P, T], U32, name="x_codes", align_bytes=64)
         nc.sync.dma_start(x_codes[:].bitcast(I32), x_words[0].rearrange("p n t -> p (n t)").bitcast(I32))
+        gn_sb = load_gain(gn, "gn_sb")
         n1_sb = load_list(n1, "n1_sb")
         gm_sb = load_gain(gm, "gm_sb")
         n3_sb = load_list(n3, "n3_sb")
@@ -74,18 +79,12 @@ def tile_picked_joinsendlerpquad_none_p_kernel(
         n5_sb = load_list(n5, "n5_sb")
         n6_sb = load_list(n6, "n6_sb")
 
-        gn_full = keep.tile([P, PACK, S], F32, name="gn_full")
-        nc.scalar.copy(gn_full[:], gn_sb[:].unsqueeze(2).to_broadcast([P, PACK, S]))
-        gn_half = keep.tile([P, PACK], F32, name="gn_half")
-        nc.vector.tensor_scalar(gn_half[:], gn_sb[:], -0.5, None, ALU.mult)
-
-        xg_codes = keep.tile([P, S], U32, name="xg_codes", align_bytes=64)
         xg_bytes = keep.tile([P, S], U8, name="xg_bytes", align_bytes=64)
         nc.vector.tensor_copy(xg_bytes[:], x_bytes[:].indirect(offs_sb[:]))
 
-        def deal(copy, raw, t0, t1, name):
+        def deal(copy, raw, t0, t1, name, tag=None, bufs=1):
             nt = t1 - t0
-            dealt = keep.tile([P, nt * P * PACK], BF16, name=name, align_bytes=64)
+            dealt = keep.tile([P, nt * P * PACK], BF16, name=name, tag=tag or name, bufs=bufs, align_bytes=64)
             copy(
                 dealt[:].rearrange("p (t m j) -> p m j t", t=nt, j=PACK),
                 raw[:].rearrange("p j (m t) -> p m j t", t=PACK)[:, :, :, t0:t1],
@@ -111,99 +110,139 @@ def tile_picked_joinsendlerpquad_none_p_kernel(
                 stop=stop,
             )
 
-        w1_lo = deal(nc.vector.tensor_copy, w1_raw, 0, 2, "w1_lo")
+        w1_lo = deal(nc.scalar.copy, w1_raw, 0, 2, "w1_lo")
         w1_hi = deal(nc.scalar.copy, w1_raw, 2, 4, "w1_hi")
-        w1_q = [quantize(w1_lo[:], "w1_lo"), quantize(w1_hi[:], "w1_hi")]
+        w1_q = [quantize(w1_lo[:], "w1_lo")]
         halves = ((0, S // 2), (S // 2, S))
+        xg = []
         for lo, hi in halves:
-            nc.vector.tensor_copy(xg_codes[:, lo:hi], x_codes[:].indirect(entries(offs_sb, lo, hi)))
+            xg_codes = keep.tile([P, hi - lo], U32, name="xg_codes%d" % lo, align_bytes=64)
+            nc.vector.tensor_copy(xg_codes[:], x_codes[:].indirect(entries(offs_sb, lo, hi)))
+            xg.append((xg_codes[:], xg_bytes[:, lo:hi]))
+        w1_q.append(quantize(w1_hi[:], "w1_hi"))
 
-        def pieces_of(t):
-            return halves if t == 0 else ((0, S),)
+        def bank(group, index, name):
+            return psum.tile([P, S], F32, name=name, tag="%s%d" % (group, index))
 
-        y_ps = [psum.tile([P, S], F32, name="y_ps%d" % t) for t in range(PACK)]
+        y_ps = [bank("a", t, "y_ps%d" % t) for t in range(PACK)]
         for t in range(PACK):
-            for lo, hi in pieces_of(t):
-                mm(y_ps[t][:, lo:hi], w1_q[t // 2], t % 2, (xg_codes[:, lo:hi], xg_bytes[:, lo:hi]), True, True)
+            for (lo, hi), picked in zip(halves, xg):
+                mm(y_ps[t][:, lo:hi], w1_q[t // 2], t % 2, picked, True, True)
 
         rows = [keep.tile([P, 2 * S], F32, name="rows%d" % t) for t in range(PACK)]
         y_gm = [keep.tile([P, S], F32, name="y_gm%d" % t) for t in range(PACK)]
+        y_gn = [keep.tile([P, S], F32, name="y_gn%d" % t) for t in range(PACK)]
         ds = [keep.tile([P, 2 * S], F32, name="ds%d" % t) for t in range(PACK)]
-        sig = [keep.tile([P, S], F32, name="sig%d" % t) for t in range(PACK)]
-        cosig = [keep.tile([P, S], F32, name="cosig%d" % t) for t in range(PACK)]
-        z_planes = keep.tile([P, PACK, S], BF16, name="z_planes")
+        sig = keep.tile([P, PACK, S], F32, name="sig")
+        cosig = keep.tile([P, PACK, S], F32, name="cosig")
 
+        for lo, hi in halves:
+            nc.vector.tensor_scalar(
+                rows[0][:, S + lo : S + hi], y_ps[0][:, lo:hi], 0.0, gn_sb[:, 0:1], ALU.max, ALU.mult
+            )
+            nc.vector.tensor_copy(ds[0][:].indirect(entries(n1_sb, lo, hi)), rows[0][:, S + lo : S + hi])
+        rl = [None] + [keep.tile([P, S], F32, name="rl%d" % t) for t in range(1, PACK)]
         for t in range(PACK):
-            for lo, hi in pieces_of(t):
-                nc.scalar.activation(rows[t][:, S + lo : S + hi], y_ps[t][:, lo:hi], ACT.Relu)
-        for t in range(PACK):
+            if t + 1 < PACK:
+                nc.scalar.activation(rl[t + 1][:], y_ps[t + 1][:], ACT.Relu)
             nc.scalar.copy(rows[t][:, :S], y_ps[t][:])
+        for t in range(1, PACK):
+            nc.gpsimd.tensor_scalar(rows[t][:, S:], rl[t][:], gn_sb[:, t : t + 1], 0.0, ALU.mult, ALU.add)
+            nc.vector.tensor_copy(ds[t][:].indirect(n1_sb[:]), rows[t][:, S:])
+        for t in range(PACK):
+            nc.gpsimd.tensor_scalar(y_gm[t][:], rows[t][:, :S], gm_sb[:, t : t + 1], 0.0, ALU.mult, ALU.add)
+        for t in range(PACK):
+            nc.gpsimd.tensor_scalar(y_gn[t][:], rows[t][:, :S], gn_sb[:, t : t + 1], -0.5, ALU.mult, ALU.mult)
         w2_b = deal(nc.scalar.copy, w2_raw, 0, 4, "w2_b")
-        w3_b = deal(nc.scalar.copy, w3_raw, 0, 4, "w3_b")
-        for t in range(PACK):
-            for lo, hi in pieces_of(t):
-                nc.vector.tensor_tensor(
-                    ds[t][:].indirect(entries(n1_sb, lo, hi)),
-                    rows[t][:, S + lo : S + hi],
-                    gn_full[:, t, lo:hi],
-                    ALU.mult,
-                )
-        for t in range(PACK):
-            nc.vector.scalar_tensor_tensor(
-                z_planes[:, t, :], rows[t][:, :S], gn_half[:, t : t + 1], ds[t][:, :S], ALU.mult, ALU.add
-            )
         w2_q = quantize(w2_b[:], "w2")
-        w3_q = quantize(w3_b[:], "w3")
         for t in range(PACK):
-            nc.scalar.activation(y_gm[t][:], y_ps[t][:], ACT.Copy, scale=gm_sb[:, t : t + 1])
-            nc.scalar.activation(sig[t][:], rows[t][:].indirect(n3_sb[:]), ACT.Sigmoid)
-            nc.scalar.activation(cosig[t][:], sig[t][:], ACT.Copy, bias=1.0, scale=-1.0)
+            nc.scalar.activation(sig[:, t, :], rows[t][:].indirect(n3_sb[:]), ACT.Sigmoid)
+            if t % 2 == 1:
+                nc.gpsimd.tensor_scalar(cosig[:, t - 1 : t + 1, :], sig[:, t - 1 : t + 1, :], -1.0, 1.0, ALU.mult, ALU.add)
+        w3_b = deal(nc.scalar.copy, w3_raw, 0, 4, "w3_b", tag="terms", bufs=3)
+        w3_q = quantize(w3_b[:], "w3")
 
-        z_q = []
-        for b, (lo, hi) in enumerate(BLOCKS):
-            z_b = keep.tile([P, (hi - lo) * PACK], BF16, name="z_b%d" % b, align_bytes=64)
+        def add_turned(dst, t, first, second):
+            cols = slice(t * P, (t + 1) * P)
+            nc.tensor.matmul(dst[:, cols], first, ident[:], start=True, stop=False, is_transpose=True)
+            nc.tensor.matmul(dst[:, cols], second, ident[:], start=False, stop=True, is_transpose=True)
+
+        def turn_back(turned, word_bank, name):
+            count = len(turned)
+            for c, src in enumerate(turned):
+                pairs = keep.tile([P, PACK * P], BF16, name="%s_pairs%d" % (name, c))
+                nc.scalar.copy(
+                    pairs[:].rearrange("j (u p e) -> j u p e", u=2, e=2),
+                    src[:].rearrange("j (u e p) -> j u p e", u=2, e=2),
+                )
+                for u in range(2):
+                    lo = (2 * c + u) * P
+                    nc.tensor.transpose(word_bank[:, lo : lo + P], pairs[:].bitcast(F32)[:, u * P : (u + 1) * P], ident[:])
+            packed = keep.tile([P, count * P * PACK], BF16, name=name + "_packed", align_bytes=64)
             nc.scalar.copy(
-                z_b[:].rearrange("p (c i t) -> p c t i", i=4, t=PACK),
-                z_planes[:, :, lo:hi].rearrange("p t (c i) -> p c t i", i=4),
+                packed[:].bitcast(F32).rearrange("p (c j u) -> p c j u", c=count, u=2),
+                word_bank[:, : count * 2 * P].rearrange("p (c u j) -> p c j u", c=count, u=2),
             )
-            z_q.append(quantize(z_b[:], "zq%d" % b))
+            return quantize(packed[:], name)
 
-        h_ps = [psum.tile([P, S], F32, name="h_ps%d" % m) for m in range(PACK)]
-        h_last = [psum.tile([P, S], F32, name="h_last%d" % m, tag="y_ps%d" % m) for m in range(PACK)]
+        z_turned = [bank("b", c, "z_turned%d" % c) for c in range(S // P)]
+        for t in range(PACK):
+            for c in range(S // P):
+                cols = slice(c * P, (c + 1) * P)
+                add_turned(z_turned[c], t, y_gn[t][:, cols], ds[t][:, cols])
+        z_halves = [turn_back(z_turned[2 * v : 2 * v + 2], bank("a", v, "z_words%d" % v), "z%d" % v) for v in range(2)]
+
+        def z_cols(lo, hi):
+            codes, scales = z_halves[lo // (S // 2)]
+            cols = slice(lo % (S // 2), lo % (S // 2) + hi - lo)
+            return codes[:, cols], scales[:, cols]
+
+        h_ps = [bank("a", m, "h_ps%d" % m) for m in range(PACK)]
         h_plain = [keep.tile([P, S], F32, name="h_plain%d" % m) for m in range(PACK)]
-        for b, (lo, hi) in enumerate(BLOCKS):
-            n = hi - lo
-            last = b == len(BLOCKS) - 1
-            banks = h_last if last else h_ps
-            part_a = keep.tile([P, PACK, n], F32, name="part_a")
-            part_b = keep.tile([P, PACK, n], F32, name="part_b")
-            for t in range(PACK):
-                nc.vector.tensor_tensor(
-                    part_a[:, t, :], y_gm[t][:].indirect(entries(n2_sb, lo, hi)), cosig[t][:, lo:hi], ALU.mult
-                )
-                nc.vector.tensor_tensor(
-                    part_b[:, t, :], y_gm[t][:].indirect(entries(n4_sb, lo, hi)), sig[t][:, lo:hi], ALU.mult
-                )
-            z2_b = keep.tile([P, n * PACK], BF16, name="z2_b%d" % b, align_bytes=64)
-            nc.vector.tensor_tensor(
-                z2_b[:].rearrange("p (c i t) -> p c t i", i=4, t=PACK),
-                part_a[:].rearrange("p t (c i) -> p c t i", i=4),
-                part_b[:].rearrange("p t (c i) -> p c t i", i=4),
-                ALU.add,
-            )
-            z2_q = quantize(z2_b[:], "z2q%d" % b)
-            if last:
-                for m in range(PACK):
-                    mm(banks[m][:, lo:hi], w2_q, m, z_q[b], True, False)
-                for m in range(PACK):
-                    mm(banks[m][:, lo:hi], w3_q, m, z2_q, False, True)
-            else:
-                for m in range(PACK):
-                    mm(banks[m][:, lo:hi], w2_q, m, z_q[b], True, False)
-                    mm(banks[m][:, lo:hi], w3_q, m, z2_q, False, True)
+
+        def gather_pair(dst_a, dst_b, t, lo, hi):
+            nc.vector.tensor_tensor(dst_a, y_gm[t][:].indirect(entries(n2_sb, lo, hi)), cosig[:, t, lo:hi], ALU.mult)
+            nc.vector.tensor_tensor(dst_b, y_gm[t][:].indirect(entries(n4_sb, lo, hi)), sig[:, t, lo:hi], ALU.mult)
+
+        def empty_h(banks, lo, hi):
             for m in range(PACK):
                 nc.scalar.copy(rows[m][:, lo:hi], banks[m][:, lo:hi])
                 nc.scalar.copy(h_plain[m][:, lo:hi], banks[m][:, lo:hi])
+
+        for b, (lo, hi) in enumerate(BLOCKS[:-1]):
+            n = hi - lo
+            turned = [bank("b", lo // P + c, "z2_turned%d" % (lo // P + c)) for c in range(n // P)]
+            for t in range(PACK):
+                terms = keep.tile([P, 2, n], F32, name="terms", bufs=3, align_bytes=64)
+                gather_pair(terms[:, 0, :], terms[:, 1, :], t, lo, hi)
+                for c in range(n // P):
+                    cols = slice(c * P, (c + 1) * P)
+                    add_turned(turned[c], t, terms[:, 0, cols], terms[:, 1, cols])
+            z2_q = turn_back(turned, bank("b", 3 if b == 0 else 0, "z2_words%d" % b), "z2q%d" % b)
+            for m in range(PACK):
+                mm(h_ps[m][:, lo:hi], w2_q, m, z_cols(lo, hi), True, False)
+                mm(h_ps[m][:, lo:hi], w3_q, m, z2_q, False, True)
+            empty_h(h_ps, lo, hi)
+
+        lo, hi = BLOCKS[-1]
+        n = hi - lo
+        terms = keep.tile([P, 2, PACK, n], F32, name="terms", bufs=3, align_bytes=64)
+        for t in range(PACK):
+            gather_pair(terms[:, 0, t, :], terms[:, 1, t, :], t, lo, hi)
+        z2_b = keep.tile([P, n * PACK], BF16, name="z2_b", align_bytes=64)
+        nc.vector.tensor_tensor(
+            z2_b[:].rearrange("p (c i t) -> p c t i", i=4, t=PACK),
+            terms[:, 0].rearrange("p t (c i) -> p c t i", i=4),
+            terms[:, 1].rearrange("p t (c i) -> p c t i", i=4),
+            ALU.add,
+        )
+        z2_q = quantize(z2_b[:], "z2_last")
+        h_last = [bank("b", (m + 1) % PACK, "h_last%d" % m) for m in range(PACK)]
+        for m in range(PACK):
+            mm(h_last[m][:, lo:hi], w2_q, m, z_cols(lo, hi), True, False)
+        for m in range(PACK):
+            mm(h_last[m][:, lo:hi], w3_q, m, z2_q, False, True)
+        empty_h(h_last, lo, hi)
 
         out_rows = out.rearrange("(p t) j -> p t j", t=PACK)
         for m in range(PACK):

@@ -50,8 +50,16 @@ def tile_picked_joinsendlerpquad_none_p_kernel(
             return lst[:, lo // LIST_ROWS : hi // LIST_ROWS]
 
         x_bytes = keep.tile([P, T], U8, name="x_bytes", align_bytes=64)
-        nc.vector.memset(x_bytes[:, : T // 2].bitcast(I32), 0)
-        nc.gpsimd.memset(x_bytes[:, T // 2 :].bitcast(I32), 0)
+        x_rows = keep.tile([P, T], U8, name="x_rows", align_bytes=64)
+        for q in range(4):
+            nc.scalar.dma_start(
+                x_rows[32 * q : 32 * q + 4, :].bitcast(I32), x_scales[0, 4 * q : 4 * q + 4, :].bitcast(I32)
+            )
+        nc.vector.memset(x_bytes[:].bitcast(I32), 0)
+        for q in range(4):
+            nc.vector.tensor_copy(
+                x_bytes[32 * q : 32 * q + 4, :].bitcast(I32), x_rows[32 * q : 32 * q + 4, :].bitcast(I32)
+            )
         warm = keep.tile([P, 1], F32, name="warm")
         nc.vector.memset(warm[:], 0.0)
         warm_out = keep.tile([P, 1], F32, name="warm_out")
@@ -60,12 +68,8 @@ def tile_picked_joinsendlerpquad_none_p_kernel(
         ident = keep.tile([P, P], F32, name="ident")
         make_identity(nc, ident[:])
 
-        w1_raw = load_weight(w1, "w1_raw")
         offs_sb = load_list(offs, "offs_sb")
-        for q in range(4):
-            nc.sync.dma_start(
-                x_bytes[32 * q : 32 * q + 4, :].bitcast(I32), x_scales[0, 4 * q : 4 * q + 4, :].bitcast(I32)
-            )
+        w1_raw = load_weight(w1, "w1_raw")
         x_codes = keep.tile([P, T], U32, name="x_codes", align_bytes=64)
         nc.sync.dma_start(x_codes[:].bitcast(I32), x_words[0].rearrange("p n t -> p (n t)").bitcast(I32))
         gn_sb = load_gain(gn, "gn_sb")
@@ -125,9 +129,11 @@ def tile_picked_joinsendlerpquad_none_p_kernel(
             return psum.tile([P, S], F32, name=name, tag="%s%d" % (group, index))
 
         y_ps = [bank("a", t, "y_ps%d" % t) for t in range(PACK)]
+        y0_rest = bank("b", 3, "y0_rest")
         for t in range(PACK):
             for (lo, hi), picked in zip(halves, xg):
-                mm(y_ps[t][:, lo:hi], w1_q[t // 2], t % 2, picked, True, True)
+                dst = y0_rest if (t == 0 and lo > 0) else y_ps[t]
+                mm(dst[:, lo:hi], w1_q[t // 2], t % 2, picked, True, True)
 
         rows = [keep.tile([P, 2 * S], F32, name="rows%d" % t) for t in range(PACK)]
         y_gm = [keep.tile([P, S], F32, name="y_gm%d" % t) for t in range(PACK)]
@@ -136,29 +142,38 @@ def tile_picked_joinsendlerpquad_none_p_kernel(
         sig = keep.tile([P, PACK, S], F32, name="sig")
         cosig = keep.tile([P, PACK, S], F32, name="cosig")
 
-        for lo, hi in halves:
-            nc.vector.tensor_scalar(
-                rows[0][:, S + lo : S + hi], y_ps[0][:, lo:hi], 0.0, gn_sb[:, 0:1], ALU.max, ALU.mult
-            )
-            nc.vector.tensor_copy(ds[0][:].indirect(entries(n1_sb, lo, hi)), rows[0][:, S + lo : S + hi])
-        rl = [None] + [keep.tile([P, S], F32, name="rl%d" % t) for t in range(1, PACK)]
+        half = S // 2
+        nc.vector.tensor_scalar(
+            rows[0][:, S : S + half], y_ps[0][:, :half], 0.0, gn_sb[:, 0:1], ALU.max, ALU.mult
+        )
+        nc.vector.tensor_copy(ds[0][:].indirect(entries(n1_sb, 0, half)), rows[0][:, S : S + half])
+        rl = [keep.tile([P, S], F32, name="rl%d" % t) for t in range(PACK)]
+        first = [half] + [0] * (PACK - 1)
+        nc.scalar.activation(rl[0][:, half:], y0_rest[:, half:], ACT.Relu)
         for t in range(PACK):
             if t + 1 < PACK:
                 nc.scalar.activation(rl[t + 1][:], y_ps[t + 1][:], ACT.Relu)
-            nc.scalar.copy(rows[t][:, :S], y_ps[t][:])
-        for t in range(1, PACK):
-            nc.gpsimd.tensor_scalar(rows[t][:, S:], rl[t][:], gn_sb[:, t : t + 1], 0.0, ALU.mult, ALU.add)
-            nc.vector.tensor_copy(ds[t][:].indirect(n1_sb[:]), rows[t][:, S:])
+            if t == 0:
+                nc.scalar.copy(rows[0][:, :half], y_ps[0][:, :half])
+                nc.scalar.copy(rows[0][:, half:S], y0_rest[:, half:])
+            else:
+                nc.scalar.copy(rows[t][:, :S], y_ps[t][:])
+        for t in range(PACK):
+            lo = first[t]
+            nc.gpsimd.tensor_scalar(
+                rows[t][:, S + lo :], rl[t][:, lo:], gn_sb[:, t : t + 1], 0.0, ALU.mult, ALU.add
+            )
+            nc.vector.tensor_copy(ds[t][:].indirect(entries(n1_sb, lo, S)), rows[t][:, S + lo :])
         for t in range(PACK):
             nc.gpsimd.tensor_scalar(y_gm[t][:], rows[t][:, :S], gm_sb[:, t : t + 1], 0.0, ALU.mult, ALU.add)
         for t in range(PACK):
             nc.gpsimd.tensor_scalar(y_gn[t][:], rows[t][:, :S], gn_sb[:, t : t + 1], -0.5, ALU.mult, ALU.mult)
-        w2_b = deal(nc.scalar.copy, w2_raw, 0, 4, "w2_b")
-        w2_q = quantize(w2_b[:], "w2")
         for t in range(PACK):
             nc.scalar.activation(sig[:, t, :], rows[t][:].indirect(n3_sb[:]), ACT.Sigmoid)
             if t % 2 == 1:
                 nc.gpsimd.tensor_scalar(cosig[:, t - 1 : t + 1, :], sig[:, t - 1 : t + 1, :], -1.0, 1.0, ALU.mult, ALU.add)
+        w2_b = deal(nc.scalar.copy, w2_raw, 0, 4, "w2_b")
+        w2_q = quantize(w2_b[:], "w2")
         w3_b = deal(nc.scalar.copy, w3_raw, 0, 4, "w3_b", tag="terms", bufs=3)
         w3_q = quantize(w3_b[:], "w3")
 
@@ -167,7 +182,7 @@ def tile_picked_joinsendlerpquad_none_p_kernel(
             nc.tensor.matmul(dst[:, cols], first, ident[:], start=True, stop=False, is_transpose=True)
             nc.tensor.matmul(dst[:, cols], second, ident[:], start=False, stop=True, is_transpose=True)
 
-        def turn_back(turned, word_bank, name):
+        def turn_back(turned, word_bank, packed, name):
             count = len(turned)
             for c, src in enumerate(turned):
                 pairs = keep.tile([P, PACK * P], BF16, name="%s_pairs%d" % (name, c))
@@ -178,19 +193,21 @@ def tile_picked_joinsendlerpquad_none_p_kernel(
                 for u in range(2):
                     lo = (2 * c + u) * P
                     nc.tensor.transpose(word_bank[:, lo : lo + P], pairs[:].bitcast(F32)[:, u * P : (u + 1) * P], ident[:])
-            packed = keep.tile([P, count * P * PACK], BF16, name=name + "_packed", align_bytes=64)
             nc.scalar.copy(
-                packed[:].bitcast(F32).rearrange("p (c j u) -> p c j u", c=count, u=2),
+                packed.rearrange("p (c j u) -> p c j u", c=count, u=2),
                 word_bank[:, : count * 2 * P].rearrange("p (c u j) -> p c j u", c=count, u=2),
             )
-            return quantize(packed[:], name)
+            return quantize(packed.bitcast(BF16), name)
 
         z_turned = [bank("b", c, "z_turned%d" % c) for c in range(S // P)]
         for t in range(PACK):
             for c in range(S // P):
                 cols = slice(c * P, (c + 1) * P)
                 add_turned(z_turned[c], t, y_gn[t][:, cols], ds[t][:, cols])
-        z_halves = [turn_back(z_turned[2 * v : 2 * v + 2], bank("a", v, "z_words%d" % v), "z%d" % v) for v in range(2)]
+        z_halves = []
+        for v in range(2):
+            z_packed = keep.tile([P, S], F32, name="z_packed%d" % v, align_bytes=64)
+            z_halves.append(turn_back(z_turned[2 * v : 2 * v + 2], bank("a", v, "z_words%d" % v), z_packed[:], "z%d" % v))
 
         def z_cols(lo, hi):
             codes, scales = z_halves[lo // (S // 2)]
@@ -209,40 +226,44 @@ def tile_picked_joinsendlerpquad_none_p_kernel(
                 nc.scalar.copy(rows[m][:, lo:hi], banks[m][:, lo:hi])
                 nc.scalar.copy(h_plain[m][:, lo:hi], banks[m][:, lo:hi])
 
-        for b, (lo, hi) in enumerate(BLOCKS[:-1]):
-            n = hi - lo
-            turned = [bank("b", lo // P + c, "z2_turned%d" % (lo // P + c)) for c in range(n // P)]
-            for t in range(PACK):
-                terms = keep.tile([P, 2, n], F32, name="terms", bufs=3, align_bytes=64)
-                gather_pair(terms[:, 0, :], terms[:, 1, :], t, lo, hi)
-                for c in range(n // P):
-                    cols = slice(c * P, (c + 1) * P)
-                    add_turned(turned[c], t, terms[:, 0, cols], terms[:, 1, cols])
-            z2_q = turn_back(turned, bank("b", 3 if b == 0 else 0, "z2_words%d" % b), "z2q%d" % b)
-            for m in range(PACK):
-                mm(h_ps[m][:, lo:hi], w2_q, m, z_cols(lo, hi), True, False)
-                mm(h_ps[m][:, lo:hi], w3_q, m, z2_q, False, True)
-            empty_h(h_ps, lo, hi)
-
-        lo, hi = BLOCKS[-1]
-        n = hi - lo
-        terms = keep.tile([P, 2, PACK, n], F32, name="terms", bufs=3, align_bytes=64)
+        turned = [bank("b", c, "z2_turned%d" % c) for c in range(half // P)]
         for t in range(PACK):
-            gather_pair(terms[:, 0, t, :], terms[:, 1, t, :], t, lo, hi)
-        z2_b = keep.tile([P, n * PACK], BF16, name="z2_b", align_bytes=64)
-        nc.vector.tensor_tensor(
-            z2_b[:].rearrange("p (c i t) -> p c t i", i=4, t=PACK),
-            terms[:, 0].rearrange("p t (c i) -> p c t i", i=4),
-            terms[:, 1].rearrange("p t (c i) -> p c t i", i=4),
-            ALU.add,
-        )
-        z2_q = quantize(z2_b[:], "z2_last")
+            terms = keep.tile([P, 2, half], F32, name="terms", bufs=3, align_bytes=64)
+            gather_pair(terms[:, 0, :], terms[:, 1, :], t, 0, half)
+            for c in range(half // P):
+                cols = slice(c * P, (c + 1) * P)
+                add_turned(turned[c], t, terms[:, 0, cols], terms[:, 1, cols])
+        late = keep.tile([P, 2 * PACK * half], F32, name="terms", bufs=3, align_bytes=64)
+        z2_q = turn_back(turned, bank("b", 3, "z2_words"), late[:, 2 * half : 4 * half], "z2_early")
+        for m in range(PACK):
+            mm(h_ps[m][:, :half], w2_q, m, z_halves[0], True, False)
+            mm(h_ps[m][:, :half], w3_q, m, z2_q, False, True)
+        empty_h(h_ps, 0, half)
+
+        for t in range(PACK):
+            gather_pair(late[:, t * half : (t + 1) * half], late[:, (PACK + t) * half : (PACK + t + 1) * half], t, half, S)
+        late_a = late[:, : PACK * half].rearrange("p (t c i) -> p c t i", t=PACK, i=4)
+        late_b = late[:, PACK * half :].rearrange("p (t c i) -> p c t i", t=PACK, i=4)
+        z2_b = [keep.tile([P, P * PACK], BF16, name="z2_b%d" % v, align_bytes=64) for v in range(2)]
+        for v in range(2):
+            runs = slice(v * P // 4, (v + 1) * P // 4)
+            nc.vector.tensor_tensor(
+                z2_b[v][:].rearrange("p (c i t) -> p c t i", i=4, t=PACK), late_a[:, runs], late_b[:, runs], ALU.add
+            )
+        z2_q = [quantize(z2_b[v][:], "z2_late%d" % v) for v in range(2)]
         h_last = [bank("b", (m + 1) % PACK, "h_last%d" % m) for m in range(PACK)]
+        lo, mid = half, half + P
         for m in range(PACK):
-            mm(h_last[m][:, lo:hi], w2_q, m, z_cols(lo, hi), True, False)
+            mm(h_last[m][:, mid:], w2_q, m, z_cols(mid, S), True, False)
         for m in range(PACK):
-            mm(h_last[m][:, lo:hi], w3_q, m, z2_q, False, True)
-        empty_h(h_last, lo, hi)
+            mm(h_ps[m][:, lo:mid], w2_q, m, z_cols(lo, mid), True, False)
+            mm(h_ps[m][:, lo:mid], w3_q, m, z2_q[0], False, True)
+            mm(h_last[m][:, mid:], w3_q, m, z2_q[1], False, True)
+        for m in range(PACK):
+            for dst in (rows[m], h_plain[m]):
+                nc.scalar.copy(dst[:, lo:mid], h_ps[m][:, lo:mid])
+            for dst in (rows[m], h_plain[m]):
+                nc.scalar.copy(dst[:, mid:S], h_last[m][:, mid:])
 
         out_rows = out.rearrange("(p t) j -> p t j", t=PACK)
         for m in range(PACK):

@@ -60,10 +60,6 @@ def tile_picked_joinsendlerpquad_none_p_kernel(
             nc.vector.tensor_copy(
                 x_bytes[32 * q : 32 * q + 4, :].bitcast(I32), x_rows[32 * q : 32 * q + 4, :].bitcast(I32)
             )
-        warm = keep.tile([P, 1], F32, name="warm")
-        nc.vector.memset(warm[:], 0.0)
-        warm_out = keep.tile([P, 1], F32, name="warm_out")
-        nc.scalar.activation(warm_out[:], warm[:], ACT.Sigmoid)
 
         ident = keep.tile([P, P], F32, name="ident")
         make_identity(nc, ident[:])
@@ -95,9 +91,9 @@ def tile_picked_joinsendlerpquad_none_p_kernel(
             )
             return dealt
 
-        def quantize(src, name):
+        def quantize(src, name, tag=None):
             width = src.shape[1] // PACK
-            codes = keep.tile([P, width], U32, name=name + "_codes", align_bytes=64)
+            codes = keep.tile([P, width], U32, name=name + "_codes", tag=tag or name + "_codes", align_bytes=64)
             scales = keep.tile([P, width], U8, name=name + "_scales", align_bytes=64)
             nc.vector.quantize_mx(out=codes[:].bitcast(FP8X4), scales=scales[:], in_=src)
             return codes[:], scales[:]
@@ -114,7 +110,7 @@ def tile_picked_joinsendlerpquad_none_p_kernel(
                 stop=stop,
             )
 
-        w1_lo = deal(nc.scalar.copy, w1_raw, 0, 2, "w1_lo")
+        w1_lo = deal(lambda dst, src: nc.scalar.activation(dst, src, ACT.Copy), w1_raw, 0, 2, "w1_lo")
         w1_hi = deal(nc.scalar.copy, w1_raw, 2, 4, "w1_hi")
         w1_q = [quantize(w1_lo[:], "w1_lo")]
         halves = ((0, S // 2), (S // 2, S))
@@ -136,7 +132,7 @@ def tile_picked_joinsendlerpquad_none_p_kernel(
                 mm(dst[:, lo:hi], w1_q[t // 2], t % 2, picked, True, True)
 
         rows = [keep.tile([P, 2 * S], F32, name="rows%d" % t) for t in range(PACK)]
-        y_gm = [keep.tile([P, S], F32, name="y_gm%d" % t) for t in range(PACK)]
+        y_gm = [keep.tile([P, S], F32, name="y_gm%d" % t, align_bytes=64) for t in range(PACK)]
         y_gn = [keep.tile([P, S], F32, name="y_gn%d" % t) for t in range(PACK)]
         ds = [keep.tile([P, 2 * S], F32, name="ds%d" % t) for t in range(PACK)]
         sig = keep.tile([P, PACK, S], F32, name="sig")
@@ -197,7 +193,7 @@ def tile_picked_joinsendlerpquad_none_p_kernel(
                 packed.rearrange("p (c j u) -> p c j u", c=count, u=2),
                 word_bank[:, : count * 2 * P].rearrange("p (c u j) -> p c j u", c=count, u=2),
             )
-            return quantize(packed.bitcast(BF16), name)
+            return packed.bitcast(BF16)
 
         z_turned = [bank("b", c, "z_turned%d" % c) for c in range(S // P)]
         for t in range(PACK):
@@ -208,11 +204,7 @@ def tile_picked_joinsendlerpquad_none_p_kernel(
         for v in range(2):
             z_packed = keep.tile([P, S], F32, name="z_packed%d" % v, align_bytes=64)
             z_halves.append(turn_back(z_turned[2 * v : 2 * v + 2], bank("a", v, "z_words%d" % v), z_packed[:], "z%d" % v))
-
-        def z_cols(lo, hi):
-            codes, scales = z_halves[lo // (S // 2)]
-            cols = slice(lo % (S // 2), lo % (S // 2) + hi - lo)
-            return codes[:, cols], scales[:, cols]
+        z_early = quantize(z_halves[0], "z_early")
 
         h_ps = [bank("a", m, "h_ps%d" % m) for m in range(PACK)]
         h_plain = [keep.tile([P, S], F32, name="h_plain%d" % m) for m in range(PACK)]
@@ -234,14 +226,19 @@ def tile_picked_joinsendlerpquad_none_p_kernel(
                 cols = slice(c * P, (c + 1) * P)
                 add_turned(turned[c], t, terms[:, 0, cols], terms[:, 1, cols])
         late = keep.tile([P, 2 * PACK * half], F32, name="terms", bufs=3, align_bytes=64)
-        z2_q = turn_back(turned, bank("b", 3, "z2_words"), late[:, 2 * half : 4 * half], "z2_early")
+        z2_q = quantize(turn_back(turned, bank("b", 3, "z2_words"), late[:, 2 * half : 4 * half], "z2"), "z2_early")
         for m in range(PACK):
-            mm(h_ps[m][:, :half], w2_q, m, z_halves[0], True, False)
+            mm(h_ps[m][:, :half], w2_q, m, z_early, True, False)
             mm(h_ps[m][:, :half], w3_q, m, z2_q, False, True)
         empty_h(h_ps, 0, half)
 
         for t in range(PACK):
             gather_pair(late[:, t * half : (t + 1) * half], late[:, (PACK + t) * half : (PACK + t + 1) * half], t, half, S)
+        z_late = quantize(z_halves[1], "z_late", tag="y_gm2")
+
+        def z_cols(lo, hi):
+            return z_late[0][:, lo - half : hi - half], z_late[1][:, lo - half : hi - half]
+
         late_a = late[:, : PACK * half].rearrange("p (t c i) -> p c t i", t=PACK, i=4)
         late_b = late[:, PACK * half :].rearrange("p (t c i) -> p c t i", t=PACK, i=4)
         z2_b = [keep.tile([P, P * PACK], BF16, name="z2_b%d" % v, align_bytes=64) for v in range(2)]
@@ -266,18 +263,20 @@ def tile_picked_joinsendlerpquad_none_p_kernel(
                 nc.scalar.copy(dst[:, mid:S], h_last[m][:, mid:])
 
         out_rows = out.rearrange("(p t) j -> p t j", t=PACK)
-        for m in range(PACK):
-            pieces = ((0, S),) if m < PACK - 1 else ((0, S // 2), (S // 2, S))
-            for lo, hi in pieces:
-                n = hi - lo
-                d5 = keep.tile([P, n], F32, name="d5_%d_%d" % (m, lo))
-                d6 = keep.tile([P, n], F32, name="d6_%d_%d" % (m, lo))
-                res = keep.tile([P, n], F32, name="res_%d_%d" % (m, lo))
-                nc.vector.tensor_tensor(
-                    d5[:], rows[m][:].indirect(entries(n5_sb, lo, hi)), h_plain[m][:, lo:hi], ALU.subtract
-                )
-                nc.vector.tensor_tensor(
-                    d6[:], rows[m][:].indirect(entries(n6_sb, lo, hi)), h_plain[m][:, lo:hi], ALU.subtract
-                )
-                nc.vector.scalar_tensor_tensor(res[:], d5[:], 0.75, d6[:], ALU.mult, ALU.mult)
-                nc.sync.dma_start(out_rows[:, m, lo:hi], res[:])
+        pieces = [(m, 0, S) for m in range(PACK - 1)] + [(PACK - 1, lo, hi) for lo, hi in halves]
+
+        def difference(lst, m, lo, hi, name):
+            dst = keep.tile([P, hi - lo], F32, name="%s_%d_%d" % (name, m, lo))
+            nc.vector.tensor_tensor(
+                dst[:], rows[m][:].indirect(entries(lst, lo, hi)), h_plain[m][:, lo:hi], ALU.subtract
+            )
+            return dst
+
+        d5 = difference(n5_sb, *pieces[0], "d5")
+        for i, (m, lo, hi) in enumerate(pieces):
+            d6 = difference(n6_sb, m, lo, hi, "d6")
+            d5_next = difference(n5_sb, *pieces[i + 1], "d5") if i + 1 < len(pieces) else None
+            res = keep.tile([P, hi - lo], F32, name="res_%d_%d" % (m, lo))
+            nc.vector.scalar_tensor_tensor(res[:], d5[:], 0.75, d6[:], ALU.mult, ALU.mult)
+            nc.sync.dma_start(out_rows[:, m, lo:hi], res[:])
+            d5 = d5_next

@@ -61,6 +61,10 @@ def tile_picked_joinsendlerpquad_none_p_kernel(
                 x_bytes[32 * q : 32 * q + 4, :].bitcast(I32), x_rows[32 * q : 32 * q + 4, :].bitcast(I32)
             )
 
+        warm = keep.tile([P, 1], F32, name="warm")
+        nc.vector.memset(warm[:], 0.0)
+        warm_out = keep.tile([P, 1], F32, name="warm_out")
+        nc.scalar.activation(warm_out[:], warm[:], ACT.Sigmoid)
         ident = keep.tile([P, P], F32, name="ident")
         make_identity(nc, ident[:])
 
@@ -110,7 +114,7 @@ def tile_picked_joinsendlerpquad_none_p_kernel(
                 stop=stop,
             )
 
-        w1_lo = deal(lambda dst, src: nc.scalar.activation(dst, src, ACT.Copy), w1_raw, 0, 2, "w1_lo")
+        w1_lo = deal(nc.scalar.copy, w1_raw, 0, 2, "w1_lo")
         w1_hi = deal(nc.scalar.copy, w1_raw, 2, 4, "w1_hi")
         w1_q = [quantize(w1_lo[:], "w1_lo")]
         halves = ((0, S // 2), (S // 2, S))

from contextlib import ExitStack

import concourse.mybir as mybir
from concourse.masks import make_identity

K, T, S, N, H = 512, 2048, 512, 512, 512
FLOPS = 2 * K * H * S + 2 * 2 * H * N * S

F32 = mybir.dt.float32
BF16 = mybir.dt.bfloat16
I32 = mybir.dt.int32
U32 = mybir.dt.uint32
U16 = mybir.dt.uint16
U8 = mybir.dt.uint8
FP8X4 = mybir.dt.float8_e4m3fn_x4
ALU = mybir.AluOpType
ACT = mybir.ActivationFunctionType

P = 128
PACK = 4
LIST_ROWS = 16
BLOCKS = ((0, 256), (256, 512))


def tile_picked_joinsendlerpquad_none_p_kernel(
    tc, x_words, x_scales, w1, gn, gm, w2, w3, offs, n1, n2, n3, n4, n5, n6, out
):
    nc = tc.nc
    with ExitStack() as ctx:
        lists = ctx.enter_context(tc.tile_pool(name="lists", bufs=1))
        keep = ctx.enter_context(tc.tile_pool(name="keep", bufs=1))
        psum = ctx.enter_context(tc.psum_pool(name="psum", bufs=1))

        def load_list(src, name):
            dst = lists.tile([P, S // LIST_ROWS], U16, name=name)
            nc.sync.dma_start(dst[:], src)
            return dst

        def load_weight(src, name):
            dst = keep.tile([P, PACK, H], F32, name=name)
            nc.sync.dma_start(dst[:], src.rearrange("(p j) c -> p j c", j=PACK))
            return dst

        def load_gain(src, name):
            dst = keep.tile([P, PACK], F32, name=name)
            nc.sync.dma_start(dst[:], src.rearrange("(p t) o -> p (t o)", t=PACK))
            return dst

        def entries(lst, lo, hi):
            return lst[:, lo // LIST_ROWS : hi // LIST_ROWS]

        x_bytes = keep.tile([P, T], U8, name="x_bytes", align_bytes=64)
        x_rows = keep.tile([P, T], U8, name="x_rows", align_bytes=64)
        for q in range(4):
            nc.scalar.dma_start(
                x_rows[32 * q : 32 * q + 4, :].bitcast(I32), x_scales[0, 4 * q : 4 * q + 4, :].bitcast(I32)
            )
        nc.vector.memset(x_bytes[:].bitcast(I32), 0)
        for q in range(4):
            nc.vector.tensor_copy(
                x_bytes[32 * q : 32 * q + 4, :].bitcast(I32), x_rows[32 * q : 32 * q + 4, :].bitcast(I32)
            )

        warm = keep.tile([P, 1], F32, name="warm")
        nc.vector.memset(warm[:], 0.0)
        warm_out = keep.tile([P, 1], F32, name="warm_out")
        nc.scalar.activation(warm_out[:], warm[:], ACT.Sigmoid)
        ident = keep.tile([P, P], F32, name="ident")
        make_identity(nc, ident[:])

        offs_sb = load_list(offs, "offs_sb")
        w1_raw = load_weight(w1, "w1_raw")
        x_codes = keep.tile([P, T], U32, name="x_codes", align_bytes=64)
        nc.sync.dma_start(x_codes[:].bitcast(I32), x_words[0].rearrange("p n t -> p (n t)").bitcast(I32))
        gn_sb = load_gain(gn, "gn_sb")
        n1_sb = load_list(n1, "n1_sb")
        gm_sb = load_gain(gm, "gm_sb")
        n3_sb = load_list(n3, "n3_sb")
        w2_raw = load_weight(w2, "w2_raw")
        w3_raw = load_weight(w3, "w3_raw")
        n2_sb = load_list(n2, "n2_sb")
        n4_sb = load_list(n4, "n4_sb")
        n5_sb = load_list(n5, "n5_sb")
        n6_sb = load_list(n6, "n6_sb")

        xg_bytes = keep.tile([P, S], U8, name="xg_bytes", align_bytes=64)
        nc.vector.tensor_copy(xg_bytes[:], x_bytes[:].indirect(offs_sb[:]))

        def deal(copy, raw, t0, t1, name, tag=None, bufs=1):
            nt = t1 - t0
            dealt = keep.tile([P, nt * P * PACK], BF16, name=name, tag=tag or name, bufs=bufs, align_bytes=64)
            copy(
                dealt[:].rearrange("p (t m j) -> p m j t", t=nt, j=PACK),
                raw[:].rearrange("p j (m t) -> p m j t", t=PACK)[:, :, :, t0:t1],
            )
            return dealt

        def quantize(src, name, tag=None):
            width = src.shape[1] // PACK
            codes = keep.tile([P, width], U32, name=name + "_codes", tag=tag or name + "_codes", align_bytes=64)
            scales = keep.tile([P, width], U8, name=name + "_scales", align_bytes=64)
            nc.vector.quantize_mx(out=codes[:].bitcast(FP8X4), scales=scales[:], in_=src)
            return codes[:], scales[:]

        def mm(dst, stationary, m, moving, start, stop):
            cols = slice(m * P, (m + 1) * P)
            nc.tensor.matmul_mx(
                out=dst,
                lhsT=stationary[0][:, cols].bitcast(FP8X4),
                lhsT_scale=stationary[1][:, cols],
                rhs=moving[0].bitcast(FP8X4),
                rhs_scale=moving[1],
                start=start,
                stop=stop,
            )

        w1_lo = deal(nc.scalar.copy, w1_raw, 0, 2, "w1_lo")
        w1_hi = deal(nc.scalar.copy, w1_raw, 2, 4, "w1_hi")
        w1_q = [quantize(w1_lo[:], "w1_lo")]
        halves = ((0, S // 2), (S // 2, S))
        xg = []
        for lo, hi in halves:
            xg_codes = keep.tile([P, hi - lo], U32, name="xg_codes%d" % lo, align_bytes=64)
            nc.vector.tensor_copy(xg_codes[:], x_codes[:].indirect(entries(offs_sb, lo, hi)))
            xg.append((xg_codes[:], xg_bytes[:, lo:hi]))
        w1_q.append(quantize(w1_hi[:], "w1_hi"))

        def bank(group, index, name):
            return psum.tile([P, S], F32, name=name, tag="%s%d" % (group, index))

        y_ps = [bank("a", t, "y_ps%d" % t) for t in range(PACK)]
        y0_rest = bank("b", 3, "y0_rest")
        for t in range(PACK):
            for (lo, hi), picked in zip(halves, xg):
                dst = y0_rest if (t == 0 and lo > 0) else y_ps[t]
                mm(dst[:, lo:hi], w1_q[t // 2], t % 2, picked, True, True)

        rows = [keep.tile([P, 2 * S], F32, name="rows%d" % t) for t in range(PACK)]
        y_gm = [keep.tile([P, S], F32, name="y_gm%d" % t, align_bytes=64) for t in range(PACK)]
        y_gn = [keep.tile([P, S], F32, name="y_gn%d" % t) for t in range(PACK)]
        ds = [keep.tile([P, 2 * S], F32, name="ds%d" % t) for t in range(PACK)]
        sig = keep.tile([P, PACK, S], F32, name="sig")
        cosig = keep.tile([P, PACK, S], F32, name="cosig")

        half = S // 2
        nc.vector.tensor_scalar(
            rows[0][:, S : S + half], y_ps[0][:, :half], 0.0, gn_sb[:, 0:1], ALU.max, ALU.mult
        )
        nc.vector.tensor_copy(ds[0][:].indirect(entries(n1_sb, 0, half)), rows[0][:, S : S + half])
        rl = [keep.tile([P, S], F32, name="rl%d" % t) for t in range(PACK)]
        first = [half] + [0] * (PACK - 1)
        nc.scalar.activation(rl[0][:, half:], y0_rest[:, half:], ACT.Relu)
        for t in range(PACK):
            if t + 1 < PACK:
                nc.scalar.activation(rl[t + 1][:], y_ps[t + 1][:], ACT.Relu)
            if t == 0:
                nc.scalar.copy(rows[0][:, :half], y_ps[0][:, :half])
                nc.scalar.copy(rows[0][:, half:S], y0_rest[:, half:])
            else:
                nc.scalar.copy(rows[t][:, :S], y_ps[t][:])
        for t in range(PACK):
            lo = first[t]
            nc.gpsimd.tensor_scalar(
                rows[t][:, S + lo :], rl[t][:, lo:], gn_sb[:, t : t + 1], 0.0, ALU.mult, ALU.add
            )
            nc.vector.tensor_copy(ds[t][:].indirect(entries(n1_sb, lo, S)), rows[t][:, S + lo :])
        for t in range(PACK):
            nc.gpsimd.tensor_scalar(y_gm[t][:], rows[t][:, :S], gm_sb[:, t : t + 1], 0.0, ALU.mult, ALU.add)
        for t in range(PACK):
            nc.gpsimd.tensor_scalar(y_gn[t][:], rows[t][:, :S], gn_sb[:, t : t + 1], -0.5, ALU.mult, ALU.mult)
        for t in range(PACK):
            nc.scalar.activation(sig[:, t, :], rows[t][:].indirect(n3_sb[:]), ACT.Sigmoid)
            if t % 2 == 1:
                nc.gpsimd.tensor_scalar(cosig[:, t - 1 : t + 1, :], sig[:, t - 1 : t + 1, :], -1.0, 1.0, ALU.mult, ALU.add)
        w2_b = deal(nc.scalar.copy, w2_raw, 0, 4, "w2_b")
        w2_q = quantize(w2_b[:], "w2")
        w3_b = deal(nc.scalar.copy, w3_raw, 0, 4, "w3_b", tag="terms", bufs=3)
        w3_q = quantize(w3_b[:], "w3")

        def add_turned(dst, t, first, second):
            cols = slice(t * P, (t + 1) * P)
            nc.tensor.matmul(dst[:, cols], first, ident[:], start=True, stop=False, is_transpose=True)
            nc.tensor.matmul(dst[:, cols], second, ident[:], start=False, stop=True, is_transpose=True)

        def turn_back(turned, word_bank, packed, name):
            count = len(turned)
            for c, src in enumerate(turned):
                pairs = keep.tile([P, PACK * P], BF16, name="%s_pairs%d" % (name, c))
                nc.scalar.copy(
                    pairs[:].rearrange("j (u p e) -> j u p e", u=2, e=2),
                    src[:].rearrange("j (u e p) -> j u p e", u=2, e=2),
                )
                for u in range(2):
                    lo = (2 * c + u) * P
                    nc.tensor.transpose(word_bank[:, lo : lo + P], pairs[:].bitcast(F32)[:, u * P : (u + 1) * P], ident[:])
            nc.scalar.copy(
                packed.rearrange("p (c j u) -> p c j u", c=count, u=2),
                word_bank[:, : count * 2 * P].rearrange("p (c u j) -> p c j u", c=count, u=2),
            )
            return packed.bitcast(BF16)

        z_turned = [bank("b", c, "z_turned%d" % c) for c in range(S // P)]
        for t in range(PACK):
            for c in range(S // P):
                cols = slice(c * P, (c + 1) * P)
                add_turned(z_turned[c], t, y_gn[t][:, cols], ds[t][:, cols])
        z_halves = []
        for v in range(2):
            z_packed = keep.tile([P, S], F32, name="z_packed%d" % v, align_bytes=64)
            z_halves.append(turn_back(z_turned[2 * v : 2 * v + 2], bank("a", v, "z_words%d" % v), z_packed[:], "z%d" % v))
        z_early = quantize(z_halves[0], "z_early")

        h_ps = [bank("a", m, "h_ps%d" % m) for m in range(PACK)]
        h_plain = [keep.tile([P, S], F32, name="h_plain%d" % m) for m in range(PACK)]

        def gather_pair(dst_a, dst_b, t, lo, hi):
            nc.vector.tensor_tensor(dst_a, y_gm[t][:].indirect(entries(n2_sb, lo, hi)), cosig[:, t, lo:hi], ALU.mult)
            nc.vector.tensor_tensor(dst_b, y_gm[t][:].indirect(entries(n4_sb, lo, hi)), sig[:, t, lo:hi], ALU.mult)

        def empty_h(banks, lo, hi):
            for m in range(PACK):
                nc.scalar.copy(rows[m][:, lo:hi], banks[m][:, lo:hi])
                nc.scalar.copy(h_plain[m][:, lo:hi], banks[m][:, lo:hi])

        turned = [bank("b", c, "z2_turned%d" % c) for c in range(half // P)]
        for t in range(PACK):
            terms = keep.tile([P, 2, half], F32, name="terms", bufs=3, align_bytes=64)
            gather_pair(terms[:, 0, :], terms[:, 1, :], t, 0, half)
            for c in range(half // P):
                cols = slice(c * P, (c + 1) * P)
                add_turned(turned[c], t, terms[:, 0, cols], terms[:, 1, cols])
        late = keep.tile([P, 2 * PACK * half], F32, name="terms", bufs=3, align_bytes=64)
        z2_q = quantize(turn_back(turned, bank("b", 3, "z2_words"), late[:, 2 * half : 4 * half], "z2"), "z2_early")
        for m in range(PACK):
            mm(h_ps[m][:, :half], w2_q, m, z_early, True, False)
            mm(h_ps[m][:, :half], w3_q, m, z2_q, False, True)
        empty_h(h_ps, 0, half)

        for t in range(PACK):
            gather_pair(late[:, t * half : (t + 1) * half], late[:, (PACK + t) * half : (PACK + t + 1) * half], t, half, S)
        z_late = quantize(z_halves[1], "z_late", tag="y_gm2")

        def z_cols(lo, hi):
            return z_late[0][:, lo - half : hi - half], z_late[1][:, lo - half : hi - half]

        late_a = late[:, : PACK * half].rearrange("p (t c i) -> p c t i", t=PACK, i=4)
        late_b = late[:, PACK * half :].rearrange("p (t c i) -> p c t i", t=PACK, i=4)
        z2_b = [keep.tile([P, P * PACK], BF16, name="z2_b%d" % v, align_bytes=64) for v in range(2)]
        for v in range(2):
            runs = slice(v * P // 4, (v + 1) * P // 4)
            nc.vector.tensor_tensor(
                z2_b[v][:].rearrange("p (c i t) -> p c t i", i=4, t=PACK), late_a[:, runs], late_b[:, runs], ALU.add
            )
        z2_q = [quantize(z2_b[v][:], "z2_late%d" % v) for v in range(2)]
        h_last = [bank("b", (m + 1) % PACK, "h_last%d" % m) for m in range(PACK)]
        lo, mid = half, half + P
        for m in range(PACK):
            mm(h_last[m][:, mid:], w2_q, m, z_cols(mid, S), True, False)
        for m in range(PACK):
            mm(h_ps[m][:, lo:mid], w2_q, m, z_cols(lo, mid), True, False)
            mm(h_ps[m][:, lo:mid], w3_q, m, z2_q[0], False, True)
            mm(h_last[m][:, mid:], w3_q, m, z2_q[1], False, True)
        for m in range(PACK):
            for dst in (rows[m], h_plain[m]):
                nc.scalar.copy(dst[:, lo:mid], h_ps[m][:, lo:mid])
            for dst in (rows[m], h_plain[m]):
                nc.scalar.copy(dst[:, mid:S], h_last[m][:, mid:])

        out_rows = out.rearrange("(p t) j -> p t j", t=PACK)
        pieces = [(m, 0, S) for m in range(PACK - 1)] + [(PACK - 1, lo, hi) for lo, hi in halves]

        def difference(lst, m, lo, hi, name):
            dst = keep.tile([P, hi - lo], F32, name="%s_%d_%d" % (name, m, lo))
            nc.vector.tensor_tensor(
                dst[:], rows[m][:].indirect(entries(lst, lo, hi)), h_plain[m][:, lo:hi], ALU.subtract
            )
            return dst

        d5 = difference(n5_sb, *pieces[0], "d5")
        for i, (m, lo, hi) in enumerate(pieces):
            d6 = difference(n6_sb, m, lo, hi, "d6")
            d5_next = difference(n5_sb, *pieces[i + 1], "d5") if i + 1 < len(pieces) else None
            res = keep.tile([P, hi - lo], F32, name="res_%d_%d" % (m, lo))
            nc.vector.scalar_tensor_tensor(res[:], d5[:], 0.75, d6[:], ALU.mult, ALU.mult)
            nc.sync.dma_start(out_rows[:, m, lo:hi], res[:])
            d5 = d5_next
